import numpy as np
import ml_dtypes


def mxq(x, axis, fmt="e4m3"):
    dtype, down = {"e4m3": (ml_dtypes.float8_e4m3fn, 7), "e5m2": (ml_dtypes.float8_e5m2, 14)}[fmt]
    v = np.moveaxis(np.asarray(x, np.float32).astype(ml_dtypes.bfloat16).astype(np.float64), axis, -1)
    blocks = v.reshape(v.shape[:-1] + (-1, 32))
    amax = np.abs(blocks).max(-1, keepdims=True)
    byte = np.maximum(np.where(amax > 0, np.frexp(amax)[1] - 1 + 127, 0) - down, 1)
    scale = np.exp2(byte - 127.0)
    codes = (blocks / scale).astype(np.float32).astype(dtype).astype(np.float64)
    return np.moveaxis((codes * scale).reshape(v.shape), -1, axis)


WIDE = False


def mx_kscale(k):
    if not WIDE:
        return np.ones(k)
    levels = np.array([10, -10, 5, -5, 0])
    if k % 512:
        return np.exp2(np.random.permutation(np.resize(levels, k // 32))).repeat(32)
    a = np.empty((k // 512, 16))
    for p in range(k // 512):
        a[p, :8] = np.random.permutation(np.resize(levels, 8))
        for g in range(8):
            far = levels[np.abs(levels - a[p, g]) >= 10]
            a[p, g + 8] = far[np.random.randint(len(far))]
    return np.exp2(a.ravel()).repeat(32)


def f64(x):
    return np.asarray(x).astype(np.float64)


def striped(idx):
    return np.tile(np.asarray(idx).reshape(-1, 16).T, (8, 1)).astype(np.uint16)


def unstriped(offs):
    return offs[:16].T.reshape(-1).astype(np.int64)


E2M1 = np.array([0.0, 0.5, 1.0, 1.5, 2.0, 3.0, 4.0, 6.0, -0.0, -0.5, -1.0, -1.5, -2.0, -3.0, -4.0, -6.0])


def pack_weight(w, fmt):
    k, n = w.shape
    w = f64(np.asarray(w, np.float32).astype(ml_dtypes.bfloat16)).reshape(k // 32, 32, n)
    amax = np.abs(w).max(1)
    if fmt == "e4m3":
        byte = np.frexp(amax)[1] - 1 + 127 - 7
    else:
        mant, ex = np.frexp(amax / 6.0)
        byte = np.where(mant > 0.5, ex, ex - 1) + 127
    byte = np.clip(np.where(amax > 0, byte, 1), 1, 254)
    scaled = (w * np.exp2(127.0 - byte)[:, None, :]).reshape(k, n).astype(np.float32)
    by_word = np.ascontiguousarray(scaled.reshape(k // 512, 128, 4, n).transpose(0, 1, 3, 2))
    if fmt == "e4m3":
        words = by_word.astype(ml_dtypes.float8_e4m3fn).view(np.uint8)
    else:
        c = by_word.astype(ml_dtypes.float4_e2m1fn).view(np.uint8) & 0xF
        words = (c[..., 0::2] | (c[..., 1::2] << 4)).reshape(k // 512, 128, 2 * n)
    return np.ascontiguousarray(words), np.ascontiguousarray(byte.astype(np.uint8).reshape(k // 512, 16, n))


def unpack_weight(words, scales, fmt):
    g, _, n = scales.shape
    words = np.ascontiguousarray(words).reshape(g, 128, n, -1)
    if fmt == "e4m3":
        vals = words.view(ml_dtypes.float8_e4m3fn).astype(np.float64)
    else:
        nib = np.empty((g, 128, n, 4), np.uint8)
        nib[..., 0::2] = words & 0xF
        nib[..., 1::2] = words >> 4
        vals = E2M1[nib]
    vals = vals * np.repeat(np.exp2(scales.astype(np.float64) - 127.0), 8, axis=1)[..., None]
    return vals.transpose(0, 1, 3, 2).reshape(g * 512, n)


D, T, I, Q, E, U, K = 512, 2048, 512, 256, 512, 1024, 32


def setup_inputs():
    n = np.random.standard_normal
    idx = np.random.permutation(T)[:I]
    idx2 = np.random.permutation(U)[:I]
    fd = mx_kscale(D)
    fi = mx_kscale(I)
    ti = np.ones(T)
    ti[idx] = fi
    keysp = pack_weight(n((D, T)) / fd[:, None], "e4m3")
    return {
        "query": (n((D, Q)) * 0.585 / np.sqrt(D) * fd[:, None]).astype(np.float32),
        "keys_words": keysp[0],
        "keys_scales": keysp[1],
        "concepts": (n((D, U)) / fd[:, None]).astype(np.float32),
        "part": np.tile(np.random.uniform(0.2, 1.0, T), (128, 1)).astype(np.float32),
        "lam": (np.random.uniform(0.7, 1.4, (Q, 1))).astype(np.float32),
        "sres": (np.random.uniform(1.0, 8.0, (I, 1))).astype(np.float32),
        "os": (np.random.uniform(4.0, 16.0, (1, I)) * fi).astype(np.float32),
        "vals": (n((E, T)) / ti).astype(np.float32),
        "memq": (np.random.uniform(0.3, 1.0, (1, Q))).astype(np.float32),
        "offs": striped(idx),
        "offs2": striped(idx2),
    }


def reference(query, keys_words, keys_scales, concepts, part, lam, sres, os, vals, memq, offs, offs2):
    idx = unstriped(offs)
    idx2 = unstriped(offs2)
    keysu = unpack_weight(keys_words, keys_scales, "e4m3")
    queryq = mxq(f64(query), 0, "e4m3")
    keysidxg = keysu[:, idx]
    a = queryq.T @ keysidxg
    conceptsidx2q = mxq(f64(concepts)[:, idx2], 0, "e4m3")
    b = queryq.T @ conceptsidx2q
    s = (a - b * f64(part)[:1][:, idx]) * f64(lam)
    p = np.exp(s)
    ptt = p.T
    rg = ptt.reshape(I, K, Q // K).sum(axis=2)
    rv0 = 1.0 / (rg + f64(sres))
    rr = np.repeat(rv0, Q // K, axis=1)
    w0 = ptt * rr
    w = w0.T
    wo1 = w * f64(os)
    wt1 = wo1.T
    vt1 = f64(vals)[:, idx].T
    vt1q = mxq(vt1, 0, "e4m3")
    wt1q = mxq(wt1, 0, "e4m3")
    o = vt1q.T @ wt1q
    o1 = np.pad(o, ((0, 0), (1, 0)))[:, :Q]
    y = o - o1 * f64(memq)
    return y

@@ -1,0 +1,241 @@
+from contextlib import ExitStack
+
+import concourse.mybir as mybir
+from concourse.masks import make_identity
+
+D, T, I, Q, E, U, K = 512, 2048, 512, 256, 512, 1024, 32
+FLOPS = 2 * D * Q * I * 2 + 2 * I * E * Q
+
+F32 = mybir.dt.float32
+BF16 = mybir.dt.bfloat16
+I32 = mybir.dt.int32
+U32 = mybir.dt.uint32
+U16 = mybir.dt.uint16
+U8 = mybir.dt.uint8
+FP8X4 = mybir.dt.float8_e4m3fn_x4
+ALU = mybir.AluOpType
+ACT = mybir.ActivationFunctionType
+AXIS = mybir.AxisListType
+
+P = 128
+PACK = 4
+GROUP = Q // K
+HALVES = Q // P
+CHUNKS = E // P
+KH = P // GROUP
+
+
+def tile_attend_withoutconcept_claimants_rowchanges_kernel(
+    tc, query, keys_words, keys_scales, concepts, part, lam, sres, slot_factor, vals, memq, offs, offs2, out
+):
+    nc = tc.nc
+    with ExitStack() as ctx:
+        sb = ctx.enter_context(tc.tile_pool(name="sb", bufs=1))
+        ps = ctx.enter_context(tc.psum_pool(name="ps", bufs=1))
+
+        def tile(shape, dtype, name):
+            return sb.tile(shape, dtype, name=name, align_bytes=64)
+
+        def bank(tag, shape, name):
+            return ps.tile(shape, F32, name=name, tag=tag)
+
+        def quantise(src, width, name):
+            codes = tile([P, width], U32, name + "_codes")
+            scales = tile([P, width], U8, name + "_scales")
+            nc.vector.quantize_mx(out=codes[:].bitcast(FP8X4), scales=scales[:], in_=src)
+            return codes, scales
+
+        def product(dst, lhs, lhs_cols, rhs):
+            nc.tensor.matmul_mx(
+                out=dst,
+                lhsT=lhs[0][:, lhs_cols].bitcast(FP8X4),
+                lhsT_scale=lhs[1][:, lhs_cols],
+                rhs=rhs[0][:].bitcast(FP8X4),
+                rhs_scale=rhs[1][:],
+                start=True,
+                stop=True,
+            )
+
+        slots = tile([P, I // 16], U16, "slots")
+        slots2 = tile([P, I // 16], U16, "slots2")
+        key_scale_pool = tile([P, T], U8, "key_scale_pool")
+        part_pool = tile([P, T], F32, "part_pool")
+        nc.vector.memset(key_scale_pool[:].bitcast(I32), 0)
+        nc.vector.memset(part_pool[:], 0.0)
+
+        nc.sync.dma_start(slots2[:], offs2)
+        query_raw = tile([P, PACK, Q], F32, "query_raw")
+        nc.sync.dma_start(query_raw[:], query.rearrange("(p t) q -> p t q", t=PACK))
+        concept_planes = concepts.rearrange("(p t) u -> t p u", t=PACK)
+        concept_pool = [tile([P, U], F32, "concept_pool%d" % t) for t in range(PACK)]
+        nc.sync.dma_start(concept_pool[0][:], concept_planes[0])
+        nc.sync.dma_start(slots[:], offs)
+        for quad in range(4):
+            nc.scalar.dma_start(
+                key_scale_pool[32 * quad : 32 * quad + 4, :].bitcast(I32),
+                keys_scales[0, 4 * quad : 4 * quad + 4, :].bitcast(I32),
+            )
+        for t in range(1, PACK):
+            nc.sync.dma_start(concept_pool[t][:], concept_planes[t])
+        nc.scalar.dma_start(part_pool[0:1, :], part[0:1, :])
+        lam_cols = tile([P, HALVES], F32, "lam_cols")
+        with nc.allow_non_contiguous_dma(reason="one score factor a partition for each half of the query rows"):
+            nc.sync.dma_start(lam_cols[:], lam.rearrange("(h p) o -> p (h o)", h=HALVES))
+        key_pool = tile([P, T], U32, "key_pool")
+        nc.sync.dma_start(key_pool[:].bitcast(I32), keys_words[0].rearrange("p n t -> p (n t)").bitcast(I32))
+        val_pool = [tile([P, T], F32, "val_pool%d" % c) for c in range(CHUNKS)]
+        reserve = tile([P, PACK], F32, "reserve")
+        nc.sync.dma_start(reserve[:], sres.rearrange("(s t) o -> s (t o)", t=PACK))
+        nc.sync.dma_start(val_pool[0][:], vals[0:P, :])
+        factor = tile([P, PACK], F32, "factor")
+        nc.sync.dma_start(factor[:], slot_factor.rearrange("o (s t) -> s (o t)", t=PACK))
+        memq_cols = tile([P, HALVES], F32, "memq_cols")
+        nc.sync.dma_start(memq_cols[:], memq.rearrange("o (p h) -> p (o h)", h=HALVES))
+        for c in range(1, CHUNKS):
+            nc.sync.dma_start(val_pool[c][:], vals[c * P : (c + 1) * P, :])
+
+        ident = tile([P, P], F32, "ident")
+        make_identity(nc, ident[:])
+
+        query_words = tile([P, Q, PACK], BF16, "query_words")
+        nc.scalar.copy(
+            query_words[:].rearrange("p (c i) t -> p c t i", i=4),
+            query_raw[:].rearrange("p t (c i) -> p c t i", i=4),
+        )
+        key_scales = tile([P, I], U8, "key_scales")
+        nc.vector.tensor_copy(key_scales[:], key_scale_pool[:].indirect(slots[:]))
+        query_mx = quantise(query_words[:].rearrange("p q t -> p (q t)"), Q, "query")
+
+        concept_listed = tile([P, PACK, I], BF16, "concept_listed")
+        half_list = I // 32
+        nc.scalar.activation(concept_listed[:, 0, :], concept_pool[0][:].indirect(slots2[:]), ACT.Copy)
+        nc.vector.tensor_copy(concept_listed[:, 1, :], concept_pool[1][:].indirect(slots2[:]))
+        nc.scalar.activation(concept_listed[:, 2, :], concept_pool[2][:].indirect(slots2[:]), ACT.Copy)
+        nc.vector.tensor_copy(concept_listed[:, 3, : I // 2], concept_pool[3][:].indirect(slots2[:, :half_list]))
+        nc.scalar.activation(concept_listed[:, 3, I // 2 :], concept_pool[3][:].indirect(slots2[:, half_list:]), ACT.Copy)
+
+        part_listed = tile([P, I], F32, "part_listed")
+        nc.vector.tensor_copy(part_listed[:], part_pool[:].indirect(slots[:]))
+        part_turned = bank("turn0", [P, PACK, P], "part_turned")
+        for t in range(PACK):
+            nc.tensor.transpose(part_turned[:, t, :], part_listed[:, t::PACK], ident[:])
+        part_cols = tile([P, PACK], F32, "part_cols")
+        nc.scalar.copy(part_cols[:], part_turned[:, :, 0])
+        part_spread = bank("turn1", [P, PACK, P], "part_spread")
+        for t in range(PACK):
+            nc.tensor.transpose(part_spread[:, t, :], part_cols[:, t : t + 1].to_broadcast([P, P]), ident[:])
+        part_rows = tile([P, PACK, P], F32, "part_rows")
+        nc.scalar.copy(part_rows[:], part_spread[:])
+
+        concept_words = tile([P, I, PACK], BF16, "concept_words")
+        split = 320
+        nc.vector.tensor_copy(
+            concept_words[:, :split, :].rearrange("p (c i) t -> p c t i", i=4),
+            concept_listed[:, :, :split].rearrange("p t (c i) -> p c t i", i=4),
+        )
+        nc.scalar.copy(
+            concept_words[:, split:, :].rearrange("p (c i) t -> p c t i", i=4),
+            concept_listed[:, :, split:].rearrange("p t (c i) -> p c t i", i=4),
+        )
+        concept_mx = quantise(concept_words[:].rearrange("p i t -> p (i t)"), I, "concept")
+
+        key_words = tile([P, I], U32, "key_words")
+        nc.vector.tensor_copy(key_words[:], key_pool[:].indirect(slots[:]))
+        key_mx = (key_words, key_scales)
+
+        b = [bank("b%d" % h, [P, I], "b%d" % h) for h in range(HALVES)]
+        a = [bank("a%d" % h, [P, I], "a%d" % h) for h in range(HALVES)]
+        for h in range(HALVES):
+            product(b[h][:], query_mx, slice(h * P, (h + 1) * P), concept_mx)
+        for h in range(HALVES):
+            product(a[h][:], query_mx, slice(h * P, (h + 1) * P), key_mx)
+
+        taken = [tile([P, PACK, P], F32, "taken%d" % h) for h in range(HALVES)]
+        for h in range(HALVES):
+            nc.vector.tensor_tensor(taken[h][:], b[h][:].rearrange("p (s t) -> p t s", t=PACK), part_rows[:], ALU.mult)
+        p_turned = []
+        for h in range(HALVES):
+            diff = tile([P, PACK, P], F32, "diff%d" % h)
+            nc.vector.tensor_tensor(diff[:], a[h][:].rearrange("p (s t) -> p t s", t=PACK), taken[h][:], ALU.subtract)
+            p = tile([P, PACK, P], F32, "p%d" % h)
+            nc.scalar.activation(p[:], diff[:], ACT.Exp, scale=lam_cols[:, h : h + 1])
+            turned = bank("b%d" % h, [P, PACK, P], "p_turned%d" % h)
+            for t in range(PACK):
+                nc.tensor.transpose(turned[:, t, :], p[:, t, :], ident[:])
+            p_turned.append(turned)
+
+        def value_operand(c, shared):
+            listed = tile([P, I], BF16, "val_listed%d" % c)
+            if shared:
+                nc.vector.tensor_copy(listed[:, : I // 2], val_pool[c][:].indirect(slots[:, :half_list]))
+                nc.scalar.activation(listed[:, I // 2 :], val_pool[c][:].indirect(slots[:, half_list:]), ACT.Copy)
+            else:
+                nc.scalar.activation(listed[:], val_pool[c][:].indirect(slots[:]), ACT.Copy)
+            pairs = listed[:].bitcast(F32)
+            turned = bank("turn%d" % (c % 2), [P, 2, P], "val_turned%d" % c)
+            for u in range(2):
+                nc.tensor.transpose(turned[:, u, :], pairs[:, u::2], ident[:])
+            words = tile([P, P * PACK], BF16, "val_words%d" % c)
+            nc.scalar.copy(words[:].bitcast(F32).rearrange("p (e u) -> p e u", u=2), turned[:].rearrange("p u e -> p e u"))
+            return quantise(words[:], P, "val%d" % c)
+
+        val_mx = [value_operand(0, False)]
+        memq_spread = bank("res0", [P, HALVES, P], "memq_spread")
+        for h in range(HALVES):
+            nc.tensor.transpose(memq_spread[:, h, :], memq_cols[:, h : h + 1].to_broadcast([P, P]), ident[:])
+        memq_rows = tile([P, Q], F32, "memq_rows")
+        nc.scalar.copy(memq_rows[:].rearrange("p (n h) -> p n h", h=HALVES), memq_spread[:].rearrange("p h n -> p n h"))
+
+
+        sums = tile([P, HALVES, PACK, KH], F32, "sums")
+        for h in range(HALVES):
+            nc.vector.tensor_reduce(
+                sums[:, h, :, :].rearrange("p t k -> p (t k)"),
+                p_turned[h][:].rearrange("p t (k j) -> p (t k) j", j=GROUP),
+                AXIS.X,
+                ALU.add,
+            )
+        shape = [P, HALVES, PACK, KH]
+        denom = tile(shape, F32, "denom")
+        nc.vector.tensor_tensor(denom[:], sums[:], reserve[:].unsqueeze(1).unsqueeze(3).broadcast_to(shape), ALU.add)
+        val_mx.append(value_operand(1, False))
+        inverse = tile(shape, F32, "inverse")
+        nc.vector.reciprocal(inverse[:], denom[:])
+        ratio = tile([P, HALVES, KH, PACK], F32, "ratio")
+        nc.vector.tensor_tensor(
+            ratio[:],
+            inverse[:].rearrange("p h t k -> p h k t"),
+            factor[:].unsqueeze(1).unsqueeze(1).broadcast_to([P, HALVES, KH, PACK]),
+            ALU.mult,
+        )
+        weight_words = tile([P, HALVES, KH, GROUP, PACK], BF16, "weight_words")
+        for h in range(HALVES):
+            nc.vector.tensor_tensor(
+                weight_words[:, h],
+                p_turned[h][:].rearrange("p t (k j) -> p k j t", j=GROUP),
+                ratio[:, h].unsqueeze(2).broadcast_to([P, KH, GROUP, PACK]),
+                ALU.mult,
+            )
+        weight_mx = quantise(weight_words[:].rearrange("p h k j t -> p (h k j t)"), Q, "weight")
+
+        def finish(first, count, tag):
+            o = bank(tag, [P, count, Q], "o%d" % first)
+            for c in range(count):
+                product(o[:, c, :], val_mx[first + c], slice(0, P), weight_mx)
+            carried = tile([P, count, Q], F32, "carried%d" % first)
+            nc.vector.memset(carried[:, :, 0:1], 0.0)
+            nc.vector.tensor_tensor(
+                carried[:, :, 1:],
+                o[:, :, : Q - 1],
+                memq_rows[:, 1:].unsqueeze(1).broadcast_to([P, count, Q - 1]),
+                ALU.mult,
+            )
+            res = tile([P, count, Q], F32, "res%d" % first)
+            nc.vector.tensor_tensor(res[:], o[:], carried[:], ALU.subtract)
+            nc.sync.dma_start(out[first * P : (first + count) * P, :].rearrange("(c p) q -> p c q", p=P), res[:])
+
+        val_mx.append(value_operand(2, False))
+        val_mx.append(value_operand(3, True))
+        finish(0, 2, "res0")
+        finish(2, 1, "res1")
+        finish(3, 1, "a0")

@@ -33,14 +33,14 @@ def tile_attend_withoutconcept_claimants_rowchanges_kernel(
         sb = ctx.enter_context(tc.tile_pool(name="sb", bufs=1))
         ps = ctx.enter_context(tc.psum_pool(name="ps", bufs=1))
 
-        def tile(shape, dtype, name):
-            return sb.tile(shape, dtype, name=name, align_bytes=64)
+        def tile(shape, dtype, name, tag=None):
+            return sb.tile(shape, dtype, name=name, tag=tag or name, align_bytes=64)
 
         def bank(tag, shape, name):
             return ps.tile(shape, F32, name=name, tag=tag)
 
-        def quantise(src, width, name):
-            codes = tile([P, width], U32, name + "_codes")
+        def quantise(src, width, name, tag=None):
+            codes = tile([P, width], U32, name + "_codes", tag)
             scales = tile([P, width], U8, name + "_scales")
             nc.vector.quantize_mx(out=codes[:].bitcast(FP8X4), scales=scales[:], in_=src)
             return codes, scales
@@ -64,58 +64,49 @@ def tile_attend_withoutconcept_claimants_rowchanges_kernel(
         nc.vector.memset(part_pool[:], 0.0)
 
         nc.sync.dma_start(slots2[:], offs2)
-        query_raw = tile([P, PACK, Q], F32, "query_raw")
-        nc.sync.dma_start(query_raw[:], query.rearrange("(p t) q -> p t q", t=PACK))
+        nc.sync.dma_start(slots[:], offs)
+        scale_rows = tile([4, 4, T // 4], I32, "scale_rows")
+        nc.sync.dma_start(scale_rows[:], keys_scales[0].bitcast(I32).rearrange("(quad r) n -> r quad n", r=4))
+        part_row = tile([1, T], F32, "part_row")
+        nc.sync.dma_start(part_row[:], part[0:1, :])
         concept_planes = concepts.rearrange("(p t) u -> t p u", t=PACK)
         concept_pool = [tile([P, U], F32, "concept_pool%d" % t) for t in range(PACK)]
-        nc.sync.dma_start(concept_pool[0][:], concept_planes[0])
-        nc.sync.dma_start(slots[:], offs)
-        for quad in range(4):
-            nc.scalar.dma_start(
-                key_scale_pool[32 * quad : 32 * quad + 4, :].bitcast(I32),
-                keys_scales[0, 4 * quad : 4 * quad + 4, :].bitcast(I32),
-            )
-        for t in range(1, PACK):
+        for t in range(PACK):
             nc.sync.dma_start(concept_pool[t][:], concept_planes[t])
-        nc.scalar.dma_start(part_pool[0:1, :], part[0:1, :])
-        lam_cols = tile([P, HALVES], F32, "lam_cols")
-        with nc.allow_non_contiguous_dma(reason="one score factor a partition for each half of the query rows"):
-            nc.sync.dma_start(lam_cols[:], lam.rearrange("(h p) o -> p (h o)", h=HALVES))
+        query_raw = tile([P, PACK, Q], F32, "query_raw")
+        nc.sync.dma_start(query_raw[:], query.rearrange("(p t) q -> p t q", t=PACK))
         key_pool = tile([P, T], U32, "key_pool")
         nc.sync.dma_start(key_pool[:].bitcast(I32), keys_words[0].rearrange("p n t -> p (n t)").bitcast(I32))
-        val_pool = [tile([P, T], F32, "val_pool%d" % c) for c in range(CHUNKS)]
         reserve = tile([P, PACK], F32, "reserve")
         nc.sync.dma_start(reserve[:], sres.rearrange("(s t) o -> s (t o)", t=PACK))
-        nc.sync.dma_start(val_pool[0][:], vals[0:P, :])
         factor = tile([P, PACK], F32, "factor")
         nc.sync.dma_start(factor[:], slot_factor.rearrange("o (s t) -> s (o t)", t=PACK))
-        memq_cols = tile([P, HALVES], F32, "memq_cols")
-        nc.sync.dma_start(memq_cols[:], memq.rearrange("o (p h) -> p (o h)", h=HALVES))
-        for c in range(1, CHUNKS):
+        val_pool = [tile([P, T], F32, "val_pool%d" % c) for c in range(CHUNKS)]
+        for c in range(CHUNKS):
             nc.sync.dma_start(val_pool[c][:], vals[c * P : (c + 1) * P, :])
 
         ident = tile([P, P], F32, "ident")
         make_identity(nc, ident[:])
+        memq_cols = tile([P, HALVES], F32, "memq_cols")
+        nc.gpsimd.dma_start(memq_cols[:], memq.rearrange("o (p h) -> p (o h)", h=HALVES))
+        lam_cols = tile([P, HALVES], F32, "lam_cols")
+        with nc.allow_non_contiguous_dma(reason="one score factor a partition for each half of the query rows"):
+            nc.gpsimd.dma_start(lam_cols[:], lam.rearrange("(h p) o -> p (h o)", h=HALVES))
 
-        query_words = tile([P, Q, PACK], BF16, "query_words")
-        nc.scalar.copy(
-            query_words[:].rearrange("p (c i) t -> p c t i", i=4),
-            query_raw[:].rearrange("p t (c i) -> p c t i", i=4),
-        )
-        key_scales = tile([P, I], U8, "key_scales")
-        nc.vector.tensor_copy(key_scales[:], key_scale_pool[:].indirect(slots[:]))
-        query_mx = quantise(query_words[:].rearrange("p q t -> p (q t)"), Q, "query")
-
-        concept_listed = tile([P, PACK, I], BF16, "concept_listed")
-        half_list = I // 32
-        nc.scalar.activation(concept_listed[:, 0, :], concept_pool[0][:].indirect(slots2[:]), ACT.Copy)
-        nc.vector.tensor_copy(concept_listed[:, 1, :], concept_pool[1][:].indirect(slots2[:]))
-        nc.scalar.activation(concept_listed[:, 2, :], concept_pool[2][:].indirect(slots2[:]), ACT.Copy)
-        nc.vector.tensor_copy(concept_listed[:, 3, : I // 2], concept_pool[3][:].indirect(slots2[:, :half_list]))
-        nc.scalar.activation(concept_listed[:, 3, I // 2 :], concept_pool[3][:].indirect(slots2[:, half_list:]), ACT.Copy)
+        nc.scalar.activation(part_pool[0:1, :], part_row[:], ACT.Copy)
+        for quad in range(4):
+            nc.vector.tensor_copy(key_scale_pool[32 * quad : 32 * quad + 4, :].bitcast(I32), scale_rows[:, quad, :])
 
         part_listed = tile([P, I], F32, "part_listed")
-        nc.vector.tensor_copy(part_listed[:], part_pool[:].indirect(slots[:]))
+        nc.scalar.activation(part_listed[:], part_pool[:].indirect(slots[:]), ACT.Copy)
+        concept_listed = tile([P, PACK, I], BF16, "concept_listed")
+        nc.vector.tensor_copy(concept_listed[:, 0, :], concept_pool[0][:].indirect(slots2[:]))
+        nc.scalar.activation(concept_listed[:, 1, :], concept_pool[1][:].indirect(slots2[:]), ACT.Copy)
+        key_scales = tile([P, I], U8, "key_scales")
+        nc.vector.tensor_copy(key_scales[:], key_scale_pool[:].indirect(slots[:]))
+        for t in range(2, PACK):
+            nc.vector.tensor_copy(concept_listed[:, t, :], concept_pool[t][:].indirect(slots2[:]))
+
         part_turned = bank("turn0", [P, PACK, P], "part_turned")
         for t in range(PACK):
             nc.tensor.transpose(part_turned[:, t, :], part_listed[:, t::PACK], ident[:])
@@ -124,11 +115,14 @@ def tile_attend_withoutconcept_claimants_rowchanges_kernel(
         part_spread = bank("turn1", [P, PACK, P], "part_spread")
         for t in range(PACK):
             nc.tensor.transpose(part_spread[:, t, :], part_cols[:, t : t + 1].to_broadcast([P, P]), ident[:])
-        part_rows = tile([P, PACK, P], F32, "part_rows")
-        nc.scalar.copy(part_rows[:], part_spread[:])
 
-        concept_words = tile([P, I, PACK], BF16, "concept_words")
-        split = 320
+        query_words = tile([P, Q, PACK], BF16, "query_words")
+        nc.scalar.copy(
+            query_words[:].rearrange("p (c i) t -> p c t i", i=4),
+            query_raw[:].rearrange("p t (c i) -> p c t i", i=4),
+        )
+        concept_words = tile([P, I, PACK], BF16, "concept_words", "query_raw")
+        split = 336
         nc.vector.tensor_copy(
             concept_words[:, :split, :].rearrange("p (c i) t -> p c t i", i=4),
             concept_listed[:, :, :split].rearrange("p t (c i) -> p c t i", i=4),
@@ -137,9 +131,18 @@ def tile_attend_withoutconcept_claimants_rowchanges_kernel(
             concept_words[:, split:, :].rearrange("p (c i) t -> p c t i", i=4),
             concept_listed[:, :, split:].rearrange("p t (c i) -> p c t i", i=4),
         )
+        query_mx = quantise(query_words[:].rearrange("p q t -> p (q t)"), Q, "query")
         concept_mx = quantise(concept_words[:].rearrange("p i t -> p (i t)"), I, "concept")
+        part_rows = tile([P, PACK, P], F32, "part_rows", "concept_listed")
+        nc.scalar.copy(part_rows[:], part_spread[:])
 
-        key_words = tile([P, I], U32, "key_words")
+        memq_spread = bank("res0", [P, HALVES, P], "memq_spread")
+        for h in range(HALVES):
+            nc.tensor.transpose(memq_spread[:, h, :], memq_cols[:, h : h + 1].to_broadcast([P, P]), ident[:])
+        memq_rows = tile([P, Q], F32, "memq_rows", "query_words")
+        nc.scalar.copy(memq_rows[:].rearrange("p (n h) -> p n h", h=HALVES), memq_spread[:].rearrange("p h n -> p n h"))
+
+        key_words = tile([P, I], U32, "key_words", "query_raw")
         nc.vector.tensor_copy(key_words[:], key_pool[:].indirect(slots[:]))
         key_mx = (key_words, key_scales)
 
@@ -150,44 +153,48 @@ def tile_attend_withoutconcept_claimants_rowchanges_kernel(
         for h in range(HALVES):
             product(a[h][:], query_mx, slice(h * P, (h + 1) * P), key_mx)
 
+        def value_gather(c, on_vector, tag=None):
+            listed = tile([P, I], BF16, "val_listed%d" % c, tag)
+            window = val_pool[c][:].indirect(slots[:])
+            if on_vector:
+                nc.vector.tensor_copy(listed[:], window)
+            else:
+                nc.scalar.activation(listed[:], window, ACT.Copy)
+            return listed
+
+        def value_words(c, listed, bank_tag, tag=None):
+            pairs = listed[:].bitcast(F32)
+            turned = bank(bank_tag, [P, 2, P], "val_turned%d" % c)
+            for u in range(2):
+                nc.tensor.transpose(turned[:, u, :], pairs[:, u::2], ident[:])
+            words = tile([P, P * PACK], BF16, "val_words%d" % c, tag)
+            nc.scalar.copy(words[:].bitcast(F32).rearrange("p (e u) -> p e u", u=2), turned[:].rearrange("p u e -> p e u"))
+            return words
+
+        listed0 = value_gather(0, False)
         taken = [tile([P, PACK, P], F32, "taken%d" % h) for h in range(HALVES)]
         for h in range(HALVES):
             nc.vector.tensor_tensor(taken[h][:], b[h][:].rearrange("p (s t) -> p t s", t=PACK), part_rows[:], ALU.mult)
+        p = tile([P, HALVES, PACK, P], F32, "p", "val_pool0")
         p_turned = []
         for h in range(HALVES):
             diff = tile([P, PACK, P], F32, "diff%d" % h)
             nc.vector.tensor_tensor(diff[:], a[h][:].rearrange("p (s t) -> p t s", t=PACK), taken[h][:], ALU.subtract)
-            p = tile([P, PACK, P], F32, "p%d" % h)
-            nc.scalar.activation(p[:], diff[:], ACT.Exp, scale=lam_cols[:, h : h + 1])
+            nc.scalar.activation(p[:, h], diff[:], ACT.Exp, scale=lam_cols[:, h : h + 1])
             turned = bank("b%d" % h, [P, PACK, P], "p_turned%d" % h)
             for t in range(PACK):
-                nc.tensor.transpose(turned[:, t, :], p[:, t, :], ident[:])
+                nc.tensor.transpose(turned[:, t, :], p[:, h, t, :], ident[:])
             p_turned.append(turned)
 
-        def value_operand(c, shared):
-            listed = tile([P, I], BF16, "val_listed%d" % c)
-            if shared:
-                nc.vector.tensor_copy(listed[:, : I // 2], val_pool[c][:].indirect(slots[:, :half_list]))
-                nc.scalar.activation(listed[:, I // 2 :], val_pool[c][:].indirect(slots[:, half_list:]), ACT.Copy)
-            else:
-                nc.scalar.activation(listed[:], val_pool[c][:].indirect(slots[:]), ACT.Copy)
-            pairs = listed[:].bitcast(F32)
-            turned = bank("turn%d" % (c % 2), [P, 2, P], "val_turned%d" % c)
-            for u in range(2):
-                nc.tensor.transpose(turned[:, u, :], pairs[:, u::2], ident[:])
-            words = tile([P, P * PACK], BF16, "val_words%d" % c)
-            nc.scalar.copy(words[:].bitcast(F32).rearrange("p (e u) -> p e u", u=2), turned[:].rearrange("p u e -> p e u"))
-            return quantise(words[:], P, "val%d" % c)
+        words0 = value_words(0, listed0, "a1")
+        listed1 = value_gather(1, True, "taken1")
+        listed2 = value_gather(2, False)
+        words1 = value_words(1, listed1, "turn0", "val_pool2")
+        listed3 = value_gather(3, False)
+        words2 = value_words(2, listed2, "turn1", "val_pool3")
+        words3 = value_words(3, listed3, "turn0")
 
-        val_mx = [value_operand(0, False)]
-        memq_spread = bank("res0", [P, HALVES, P], "memq_spread")
-        for h in range(HALVES):
-            nc.tensor.transpose(memq_spread[:, h, :], memq_cols[:, h : h + 1].to_broadcast([P, P]), ident[:])
-        memq_rows = tile([P, Q], F32, "memq_rows")
-        nc.scalar.copy(memq_rows[:].rearrange("p (n h) -> p n h", h=HALVES), memq_spread[:].rearrange("p h n -> p n h"))
-
-
-        sums = tile([P, HALVES, PACK, KH], F32, "sums")
+        sums = tile([P, HALVES, PACK, KH], F32, "sums", "val_pool1")
         for h in range(HALVES):
             nc.vector.tensor_reduce(
                 sums[:, h, :, :].rearrange("p t k -> p (t k)"),
@@ -198,7 +205,7 @@ def tile_attend_withoutconcept_claimants_rowchanges_kernel(
         shape = [P, HALVES, PACK, KH]
         denom = tile(shape, F32, "denom")
         nc.vector.tensor_tensor(denom[:], sums[:], reserve[:].unsqueeze(1).unsqueeze(3).broadcast_to(shape), ALU.add)
-        val_mx.append(value_operand(1, False))
+        val_mx = [quantise(words0[:], P, "val0", "val_pool1")]
         inverse = tile(shape, F32, "inverse")
         nc.vector.reciprocal(inverse[:], denom[:])
         ratio = tile([P, HALVES, KH, PACK], F32, "ratio")
@@ -216,6 +223,7 @@ def tile_attend_withoutconcept_claimants_rowchanges_kernel(
                 ratio[:, h].unsqueeze(2).broadcast_to([P, KH, GROUP, PACK]),
                 ALU.mult,
             )
+        val_mx.append(quantise(words1[:], P, "val1", "ratio"))
         weight_mx = quantise(weight_words[:].rearrange("p h k j t -> p (h k j t)"), Q, "weight")
 
         def finish(first, count, tag):
@@ -234,8 +242,7 @@ def tile_attend_withoutconcept_claimants_rowchanges_kernel(
             nc.vector.tensor_tensor(res[:], o[:], carried[:], ALU.subtract)
             nc.sync.dma_start(out[first * P : (first + count) * P, :].rearrange("(c p) q -> p c q", p=P), res[:])
 
-        val_mx.append(value_operand(2, False))
-        val_mx.append(value_operand(3, True))
+        val_mx.append(quantise(words2[:], P, "val2", "weight_words"))
+        val_mx.append(quantise(words3[:], P, "val3", "val_pool2"))
         finish(0, 2, "res0")
-        finish(2, 1, "res1")
-        finish(3, 1, "a0")
+        finish(2, 2, "res1")

@@ -65,8 +65,10 @@ def tile_attend_withoutconcept_claimants_rowchanges_kernel(
 
         nc.sync.dma_start(slots2[:], offs2)
         nc.sync.dma_start(slots[:], offs)
-        scale_rows = tile([4, 4, T // 4], I32, "scale_rows")
-        nc.sync.dma_start(scale_rows[:], keys_scales[0].bitcast(I32).rearrange("(quad r) n -> r quad n", r=4))
+        scale_rows = tile([P, 2, T // 4], I32, "scale_rows")
+        scale_source = keys_scales[0].bitcast(I32).rearrange("(half quad r) n -> half r quad n", half=2, r=4)
+        nc.sync.dma_start(scale_rows[0:4], scale_source[0])
+        nc.scalar.dma_start(scale_rows[64:68], scale_source[1])
         part_row = tile([1, T], F32, "part_row")
         nc.sync.dma_start(part_row[:], part[0:1, :])
         concept_planes = concepts.rearrange("(p t) u -> t p u", t=PACK)
@@ -95,7 +97,7 @@ def tile_attend_withoutconcept_claimants_rowchanges_kernel(
 
         nc.scalar.activation(part_pool[0:1, :], part_row[:], ACT.Copy)
         for quad in range(4):
-            nc.vector.tensor_copy(key_scale_pool[32 * quad : 32 * quad + 4, :].bitcast(I32), scale_rows[:, quad, :])
+            nc.vector.tensor_copy(key_scale_pool[32 * quad : 32 * quad + 4, :].bitcast(I32), scale_rows[64 * (quad // 2) : 64 * (quad // 2) + 4, quad % 2, :])
 
         part_listed = tile([P, I], F32, "part_listed")
         nc.scalar.activation(part_listed[:], part_pool[:].indirect(slots[:]), ACT.Copy)
@@ -121,20 +123,15 @@ def tile_attend_withoutconcept_claimants_rowchanges_kernel(
             query_words[:].rearrange("p (c i) t -> p c t i", i=4),
             query_raw[:].rearrange("p t (c i) -> p c t i", i=4),
         )
-        concept_words = tile([P, I, PACK], BF16, "concept_words", "query_raw")
-        split = 336
-        nc.vector.tensor_copy(
-            concept_words[:, :split, :].rearrange("p (c i) t -> p c t i", i=4),
-            concept_listed[:, :, :split].rearrange("p t (c i) -> p c t i", i=4),
-        )
-        nc.scalar.copy(
-            concept_words[:, split:, :].rearrange("p (c i) t -> p c t i", i=4),
-            concept_listed[:, :, split:].rearrange("p t (c i) -> p c t i", i=4),
-        )
-        query_mx = quantise(query_words[:].rearrange("p q t -> p (q t)"), Q, "query")
-        concept_mx = quantise(concept_words[:].rearrange("p i t -> p (i t)"), I, "concept")
-        part_rows = tile([P, PACK, P], F32, "part_rows", "concept_listed")
+        part_rows = tile([P, PACK, P], F32, "part_rows", "query_raw")
         nc.scalar.copy(part_rows[:], part_spread[:])
+        concept_words = tile([P, I, PACK], BF16, "concept_words")
+        nc.vector.tensor_copy(
+            concept_words[:].rearrange("p (c i) t -> p c t i", i=4),
+            concept_listed[:].rearrange("p t (c i) -> p c t i", i=4),
+        )
+        concept_mx = quantise(concept_words[:].rearrange("p i t -> p (i t)"), I, "concept")
+        query_mx = quantise(query_words[:].rearrange("p q t -> p (q t)"), Q, "query")
 
         memq_spread = bank("res0", [P, HALVES, P], "memq_spread")
         for h in range(HALVES):
@@ -142,7 +139,7 @@ def tile_attend_withoutconcept_claimants_rowchanges_kernel(
         memq_rows = tile([P, Q], F32, "memq_rows", "query_words")
         nc.scalar.copy(memq_rows[:].rearrange("p (n h) -> p n h", h=HALVES), memq_spread[:].rearrange("p h n -> p n h"))
 
-        key_words = tile([P, I], U32, "key_words", "query_raw")
+        key_words = tile([P, I], U32, "key_words", "concept_words")
         nc.vector.tensor_copy(key_words[:], key_pool[:].indirect(slots[:]))
         key_mx = (key_words, key_scales)
 
@@ -186,7 +183,7 @@ def tile_attend_withoutconcept_claimants_rowchanges_kernel(
                 nc.tensor.transpose(turned[:, t, :], p[:, h, t, :], ident[:])
             p_turned.append(turned)
 
-        words0 = value_words(0, listed0, "a1")
+        words0 = value_words(0, listed0, "res1", "diff1")
         listed1 = value_gather(1, True, "taken1")
         listed2 = value_gather(2, False)
         words1 = value_words(1, listed1, "turn0", "val_pool2")
@@ -224,7 +221,7 @@ def tile_attend_withoutconcept_claimants_rowchanges_kernel(
                 ALU.mult,
             )
         val_mx.append(quantise(words1[:], P, "val1", "ratio"))
-        weight_mx = quantise(weight_words[:].rearrange("p h k j t -> p (h k j t)"), Q, "weight")
+        weight_mx = quantise(weight_words[:].rearrange("p h k j t -> p (h k j t)"), Q, "weight", "val_listed3")
 
         def finish(first, count, tag):
             o = bank(tag, [P, count, Q], "o%d" % first)

@@ -130,8 +130,8 @@ def tile_attend_withoutconcept_claimants_rowchanges_kernel(
             concept_words[:].rearrange("p (c i) t -> p c t i", i=4),
             concept_listed[:].rearrange("p t (c i) -> p c t i", i=4),
         )
+        query_mx = quantise(query_words[:].rearrange("p q t -> p (q t)"), Q, "query", "concept_listed")
         concept_mx = quantise(concept_words[:].rearrange("p i t -> p (i t)"), I, "concept")
-        query_mx = quantise(query_words[:].rearrange("p q t -> p (q t)"), Q, "query")
 
         memq_spread = bank("res0", [P, HALVES, P], "memq_spread")
         for h in range(HALVES):
@@ -186,7 +186,7 @@ def tile_attend_withoutconcept_claimants_rowchanges_kernel(
         words0 = value_words(0, listed0, "res1", "diff1")
         listed1 = value_gather(1, True, "taken1")
         listed2 = value_gather(2, False)
-        words1 = value_words(1, listed1, "turn0", "val_pool2")
+        words1 = value_words(1, listed1, "res1", "val_pool2")
         listed3 = value_gather(3, False)
         words2 = value_words(2, listed2, "turn1", "val_pool3")
         words3 = value_words(3, listed3, "turn0")
@@ -205,6 +205,7 @@ def tile_attend_withoutconcept_claimants_rowchanges_kernel(
         val_mx = [quantise(words0[:], P, "val0", "val_pool1")]
         inverse = tile(shape, F32, "inverse")
         nc.vector.reciprocal(inverse[:], denom[:])
+        val_mx.append(quantise(words1[:], P, "val1", "denom"))
         ratio = tile([P, HALVES, KH, PACK], F32, "ratio")
         nc.vector.tensor_tensor(
             ratio[:],
@@ -220,7 +221,7 @@ def tile_attend_withoutconcept_claimants_rowchanges_kernel(
                 ratio[:, h].unsqueeze(2).broadcast_to([P, KH, GROUP, PACK]),
                 ALU.mult,
             )
-        val_mx.append(quantise(words1[:], P, "val1", "ratio"))
+        val_mx.append(quantise(words2[:], P, "val2", "ratio"))
         weight_mx = quantise(weight_words[:].rearrange("p h k j t -> p (h k j t)"), Q, "weight", "val_listed3")
 
         def finish(first, count, tag):
@@ -239,7 +240,6 @@ def tile_attend_withoutconcept_claimants_rowchanges_kernel(
             nc.vector.tensor_tensor(res[:], o[:], carried[:], ALU.subtract)
             nc.sync.dma_start(out[first * P : (first + count) * P, :].rearrange("(c p) q -> p c q", p=P), res[:])
 
-        val_mx.append(quantise(words2[:], P, "val2", "weight_words"))
-        val_mx.append(quantise(words3[:], P, "val3", "val_pool2"))
+        val_mx.append(quantise(words3[:], P, "val3", "weight_words"))
         finish(0, 2, "res0")
         finish(2, 2, "res1")

from contextlib import ExitStack

import concourse.mybir as mybir
from concourse.masks import make_identity

D, T, I, Q, E, U, K = 512, 2048, 512, 256, 512, 1024, 32
FLOPS = 2 * D * Q * I * 2 + 2 * I * E * Q

F32 = mybir.dt.float32
BF16 = mybir.dt.bfloat16
I32 = mybir.dt.int32
U32 = mybir.dt.uint32
U16 = mybir.dt.uint16
U8 = mybir.dt.uint8
FP8X4 = mybir.dt.float8_e4m3fn_x4
ALU = mybir.AluOpType
ACT = mybir.ActivationFunctionType
AXIS = mybir.AxisListType

P = 128
PACK = 4
GROUP = Q // K
HALVES = Q // P
CHUNKS = E // P
KH = P // GROUP


def tile_attend_withoutconcept_claimants_rowchanges_kernel(
    tc, query, keys_words, keys_scales, concepts, part, lam, sres, slot_factor, vals, memq, offs, offs2, out
):
    nc = tc.nc
    with ExitStack() as ctx:
        sb = ctx.enter_context(tc.tile_pool(name="sb", bufs=1))
        ps = ctx.enter_context(tc.psum_pool(name="ps", bufs=1))

        def tile(shape, dtype, name, tag=None):
            return sb.tile(shape, dtype, name=name, tag=tag or name, align_bytes=64)

        def bank(tag, shape, name):
            return ps.tile(shape, F32, name=name, tag=tag)

        def quantise(src, width, name, tag=None):
            codes = tile([P, width], U32, name + "_codes", tag)
            scales = tile([P, width], U8, name + "_scales")
            nc.vector.quantize_mx(out=codes[:].bitcast(FP8X4), scales=scales[:], in_=src)
            return codes, scales

        def product(dst, lhs, lhs_cols, rhs):
            nc.tensor.matmul_mx(
                out=dst,
                lhsT=lhs[0][:, lhs_cols].bitcast(FP8X4),
                lhsT_scale=lhs[1][:, lhs_cols],
                rhs=rhs[0][:].bitcast(FP8X4),
                rhs_scale=rhs[1][:],
                start=True,
                stop=True,
            )

        slots = tile([P, I // 16], U16, "slots")
        slots2 = tile([P, I // 16], U16, "slots2")
        key_scale_pool = tile([P, T], U8, "key_scale_pool")
        part_pool = tile([P, T], F32, "part_pool")
        nc.vector.memset(key_scale_pool[:].bitcast(I32), 0)
        nc.vector.memset(part_pool[:], 0.0)

        nc.sync.dma_start(slots2[:], offs2)
        nc.sync.dma_start(slots[:], offs)
        scale_rows = tile([P, 2, T // 4], I32, "scale_rows")
        scale_source = keys_scales[0].bitcast(I32).rearrange("(half quad r) n -> half r quad n", half=2, r=4)
        nc.sync.dma_start(scale_rows[0:4], scale_source[0])
        nc.scalar.dma_start(scale_rows[64:68], scale_source[1])
        part_row = tile([1, T], F32, "part_row")
        nc.sync.dma_start(part_row[:], part[0:1, :])
        concept_planes = concepts.rearrange("(p t) u -> t p u", t=PACK)
        concept_pool = [tile([P, U], F32, "concept_pool%d" % t) for t in range(PACK)]
        for t in range(PACK):
            nc.sync.dma_start(concept_pool[t][:], concept_planes[t])
        query_raw = tile([P, PACK, Q], F32, "query_raw")
        nc.sync.dma_start(query_raw[:], query.rearrange("(p t) q -> p t q", t=PACK))
        key_pool = tile([P, T], U32, "key_pool")
        nc.sync.dma_start(key_pool[:].bitcast(I32), keys_words[0].rearrange("p n t -> p (n t)").bitcast(I32))
        reserve = tile([P, PACK], F32, "reserve")
        nc.sync.dma_start(reserve[:], sres.rearrange("(s t) o -> s (t o)", t=PACK))
        factor = tile([P, PACK], F32, "factor")
        nc.sync.dma_start(factor[:], slot_factor.rearrange("o (s t) -> s (o t)", t=PACK))
        val_pool = [tile([P, T], F32, "val_pool%d" % c) for c in range(CHUNKS)]
        for c in range(CHUNKS):
            nc.sync.dma_start(val_pool[c][:], vals[c * P : (c + 1) * P, :])

        ident = tile([P, P], F32, "ident")
        make_identity(nc, ident[:])
        memq_cols = tile([P, HALVES], F32, "memq_cols")
        nc.gpsimd.dma_start(memq_cols[:], memq.rearrange("o (p h) -> p (o h)", h=HALVES))
        lam_cols = tile([P, HALVES], F32, "lam_cols")
        with nc.allow_non_contiguous_dma(reason="one score factor a partition for each half of the query rows"):
            nc.gpsimd.dma_start(lam_cols[:], lam.rearrange("(h p) o -> p (h o)", h=HALVES))

        nc.scalar.activation(part_pool[0:1, :], part_row[:], ACT.Copy)
        for quad in range(4):
            nc.vector.tensor_copy(key_scale_pool[32 * quad : 32 * quad + 4, :].bitcast(I32), scale_rows[64 * (quad // 2) : 64 * (quad // 2) + 4, quad % 2, :])

        part_listed = tile([P, I], F32, "part_listed")
        nc.scalar.activation(part_listed[:], part_pool[:].indirect(slots[:]), ACT.Copy)
        concept_listed = tile([P, PACK, I], BF16, "concept_listed")
        nc.vector.tensor_copy(concept_listed[:, 0, :], concept_pool[0][:].indirect(slots2[:]))
        nc.scalar.activation(concept_listed[:, 1, :], concept_pool[1][:].indirect(slots2[:]), ACT.Copy)
        key_scales = tile([P, I], U8, "key_scales")
        nc.vector.tensor_copy(key_scales[:], key_scale_pool[:].indirect(slots[:]))
        for t in range(2, PACK):
            nc.vector.tensor_copy(concept_listed[:, t, :], concept_pool[t][:].indirect(slots2[:]))

        part_turned = bank("turn0", [P, PACK, P], "part_turned")
        for t in range(PACK):
            nc.tensor.transpose(part_turned[:, t, :], part_listed[:, t::PACK], ident[:])
        part_cols = tile([P, PACK], F32, "part_cols")
        nc.scalar.copy(part_cols[:], part_turned[:, :, 0])
        part_spread = bank("turn1", [P, PACK, P], "part_spread")
        for t in range(PACK):
            nc.tensor.transpose(part_spread[:, t, :], part_cols[:, t : t + 1].to_broadcast([P, P]), ident[:])

        query_words = tile([P, Q, PACK], BF16, "query_words")
        nc.scalar.copy(
            query_words[:].rearrange("p (c i) t -> p c t i", i=4),
            query_raw[:].rearrange("p t (c i) -> p c t i", i=4),
        )
        part_rows = tile([P, PACK, P], F32, "part_rows", "query_raw")
        nc.scalar.copy(part_rows[:], part_spread[:])
        concept_words = tile([P, I, PACK], BF16, "concept_words")
        nc.vector.tensor_copy(
            concept_words[:].rearrange("p (c i) t -> p c t i", i=4),
            concept_listed[:].rearrange("p t (c i) -> p c t i", i=4),
        )
        query_mx = quantise(query_words[:].rearrange("p q t -> p (q t)"), Q, "query", "concept_listed")
        concept_mx = quantise(concept_words[:].rearrange("p i t -> p (i t)"), I, "concept")

        memq_spread = bank("res0", [P, HALVES, P], "memq_spread")
        for h in range(HALVES):
            nc.tensor.transpose(memq_spread[:, h, :], memq_cols[:, h : h + 1].to_broadcast([P, P]), ident[:])
        memq_rows = tile([P, Q], F32, "memq_rows", "query_words")
        nc.scalar.copy(memq_rows[:].rearrange("p (n h) -> p n h", h=HALVES), memq_spread[:].rearrange("p h n -> p n h"))

        key_words = tile([P, I], U32, "key_words", "concept_words")
        nc.vector.tensor_copy(key_words[:], key_pool[:].indirect(slots[:]))
        key_mx = (key_words, key_scales)

        b = [bank("b%d" % h, [P, I], "b%d" % h) for h in range(HALVES)]
        a = [bank("a%d" % h, [P, I], "a%d" % h) for h in range(HALVES)]
        for h in range(HALVES):
            product(b[h][:], query_mx, slice(h * P, (h + 1) * P), concept_mx)
        for h in range(HALVES):
            product(a[h][:], query_mx, slice(h * P, (h + 1) * P), key_mx)

        def value_gather(c, on_vector, tag=None):
            listed = tile([P, I], BF16, "val_listed%d" % c, tag)
            window = val_pool[c][:].indirect(slots[:])
            if on_vector:
                nc.vector.tensor_copy(listed[:], window)
            else:
                nc.scalar.activation(listed[:], window, ACT.Copy)
            return listed

        def value_words(c, listed, bank_tag, tag=None):
            pairs = listed[:].bitcast(F32)
            turned = bank(bank_tag, [P, 2, P], "val_turned%d" % c)
            for u in range(2):
                nc.tensor.transpose(turned[:, u, :], pairs[:, u::2], ident[:])
            words = tile([P, P * PACK], BF16, "val_words%d" % c, tag)
            nc.scalar.copy(words[:].bitcast(F32).rearrange("p (e u) -> p e u", u=2), turned[:].rearrange("p u e -> p e u"))
            return words

        listed0 = value_gather(0, False)
        taken = [tile([P, PACK, P], F32, "taken%d" % h) for h in range(HALVES)]
        for h in range(HALVES):
            nc.vector.tensor_tensor(taken[h][:], b[h][:].rearrange("p (s t) -> p t s", t=PACK), part_rows[:], ALU.mult)
        p = tile([P, HALVES, PACK, P], F32, "p", "val_pool0")
        p_turned = []
        for h in range(HALVES):
            diff = tile([P, PACK, P], F32, "diff%d" % h)
            nc.vector.tensor_tensor(diff[:], a[h][:].rearrange("p (s t) -> p t s", t=PACK), taken[h][:], ALU.subtract)
            nc.scalar.activation(p[:, h], diff[:], ACT.Exp, scale=lam_cols[:, h : h + 1])
            turned = bank("b%d" % h, [P, PACK, P], "p_turned%d" % h)
            for t in range(PACK):
                nc.tensor.transpose(turned[:, t, :], p[:, h, t, :], ident[:])
            p_turned.append(turned)

        words0 = value_words(0, listed0, "res1", "diff1")
        listed1 = value_gather(1, True, "taken1")
        listed2 = value_gather(2, False)
        words1 = value_words(1, listed1, "res1", "val_pool2")
        listed3 = value_gather(3, False)
        words2 = value_words(2, listed2, "turn1", "val_pool3")
        words3 = value_words(3, listed3, "turn0")

        sums = tile([P, HALVES, PACK, KH], F32, "sums", "val_pool1")
        for h in range(HALVES):
            nc.vector.tensor_reduce(
                sums[:, h, :, :].rearrange("p t k -> p (t k)"),
                p_turned[h][:].rearrange("p t (k j) -> p (t k) j", j=GROUP),
                AXIS.X,
                ALU.add,
            )
        shape = [P, HALVES, PACK, KH]
        denom = tile(shape, F32, "denom")
        nc.vector.tensor_tensor(denom[:], sums[:], reserve[:].unsqueeze(1).unsqueeze(3).broadcast_to(shape), ALU.add)
        val_mx = [quantise(words0[:], P, "val0", "val_pool1")]
        inverse = tile(shape, F32, "inverse")
        nc.vector.reciprocal(inverse[:], denom[:])
        val_mx.append(quantise(words1[:], P, "val1", "denom"))
        ratio = tile([P, HALVES, KH, PACK], F32, "ratio")
        nc.vector.tensor_tensor(
            ratio[:],
            inverse[:].rearrange("p h t k -> p h k t"),
            factor[:].unsqueeze(1).unsqueeze(1).broadcast_to([P, HALVES, KH, PACK]),
            ALU.mult,
        )
        weight_words = tile([P, HALVES, KH, GROUP, PACK], BF16, "weight_words")
        for h in range(HALVES):
            nc.vector.tensor_tensor(
                weight_words[:, h],
                p_turned[h][:].rearrange("p t (k j) -> p k j t", j=GROUP),
                ratio[:, h].unsqueeze(2).broadcast_to([P, KH, GROUP, PACK]),
                ALU.mult,
            )
        val_mx.append(quantise(words2[:], P, "val2", "ratio"))
        weight_mx = quantise(weight_words[:].rearrange("p h k j t -> p (h k j t)"), Q, "weight", "val_listed3")

        def finish(first, count, tag):
            o = bank(tag, [P, count, Q], "o%d" % first)
            for c in range(count):
                product(o[:, c, :], val_mx[first + c], slice(0, P), weight_mx)
            carried = tile([P, count, Q], F32, "carried%d" % first)
            nc.vector.memset(carried[:, :, 0:1], 0.0)
            nc.vector.tensor_tensor(
                carried[:, :, 1:],
                o[:, :, : Q - 1],
                memq_rows[:, 1:].unsqueeze(1).broadcast_to([P, count, Q - 1]),
                ALU.mult,
            )
            res = tile([P, count, Q], F32, "res%d" % first)
            nc.vector.tensor_tensor(res[:], o[:], carried[:], ALU.subtract)
            nc.sync.dma_start(out[first * P : (first + count) * P, :].rearrange("(c p) q -> p c q", p=P), res[:])

        val_mx.append(quantise(words3[:], P, "val3", "weight_words"))
        finish(0, 2, "res0")
        finish(2, 2, "res1")
